import numpy as np
import ml_dtypes


def mxq(x, axis, fmt="e4m3"):
    dtype, down = {"e4m3": (ml_dtypes.float8_e4m3fn, 7), "e5m2": (ml_dtypes.float8_e5m2, 14)}[fmt]
    v = np.moveaxis(np.asarray(x, np.float32).astype(ml_dtypes.bfloat16).astype(np.float64), axis, -1)
    blocks = v.reshape(v.shape[:-1] + (-1, 32))
    amax = np.abs(blocks).max(-1, keepdims=True)
    byte = np.maximum(np.where(amax > 0, np.frexp(amax)[1] - 1 + 127, 0) - down, 1)
    scale = np.exp2(byte - 127.0)
    codes = (blocks / scale).astype(np.float32).astype(dtype).astype(np.float64)
    return np.moveaxis((codes * scale).reshape(v.shape), -1, axis)


WIDE = False


def mx_kscale(k):
    if not WIDE:
        return np.ones(k)
    levels = np.array([10, -10, 5, -5, 0])
    if k % 512:
        return np.exp2(np.random.permutation(np.resize(levels, k // 32))).repeat(32)
    a = np.empty((k // 512, 16))
    for p in range(k // 512):
        a[p, :8] = np.random.permutation(np.resize(levels, 8))
        for g in range(8):
            far = levels[np.abs(levels - a[p, g]) >= 10]
            a[p, g + 8] = far[np.random.randint(len(far))]
    return np.exp2(a.ravel()).repeat(32)


def f64(x):
    return np.asarray(x).astype(np.float64)


def striped(idx):
    return np.tile(np.asarray(idx).reshape(-1, 16).T, (8, 1)).astype(np.uint16)


def unstriped(offs):
    return offs[:16].T.reshape(-1).astype(np.int64)


E2M1 = np.array([0.0, 0.5, 1.0, 1.5, 2.0, 3.0, 4.0, 6.0, -0.0, -0.5, -1.0, -1.5, -2.0, -3.0, -4.0, -6.0])


def pack_weight(w, fmt):
    k, n = w.shape
    w = f64(np.asarray(w, np.float32).astype(ml_dtypes.bfloat16)).reshape(k // 32, 32, n)
    amax = np.abs(w).max(1)
    if fmt == "e4m3":
        byte = np.frexp(amax)[1] - 1 + 127 - 7
    else:
        mant, ex = np.frexp(amax / 6.0)
        byte = np.where(mant > 0.5, ex, ex - 1) + 127
    byte = np.clip(np.where(amax > 0, byte, 1), 1, 254)
    scaled = (w * np.exp2(127.0 - byte)[:, None, :]).reshape(k, n).astype(np.float32)
    by_word = np.ascontiguousarray(scaled.reshape(k // 512, 128, 4, n).transpose(0, 1, 3, 2))
    if fmt == "e4m3":
        words = by_word.astype(ml_dtypes.float8_e4m3fn).view(np.uint8)
    else:
        c = by_word.astype(ml_dtypes.float4_e2m1fn).view(np.uint8) & 0xF
        words = (c[..., 0::2] | (c[..., 1::2] << 4)).reshape(k // 512, 128, 2 * n)
    return np.ascontiguousarray(words), np.ascontiguousarray(byte.astype(np.uint8).reshape(k // 512, 16, n))


def unpack_weight(words, scales, fmt):
    g, _, n = scales.shape
    words = np.ascontiguousarray(words).reshape(g, 128, n, -1)
    if fmt == "e4m3":
        vals = words.view(ml_dtypes.float8_e4m3fn).astype(np.float64)
    else:
        nib = np.empty((g, 128, n, 4), np.uint8)
        nib[..., 0::2] = words & 0xF
        nib[..., 1::2] = words >> 4
        vals = E2M1[nib]
    vals = vals * np.repeat(np.exp2(scales.astype(np.float64) - 127.0), 8, axis=1)[..., None]
    return vals.transpose(0, 1, 3, 2).reshape(g * 512, n)


D, T, I, G, U, Q = 512, 4096, 2048, 512, 1024, 128


def setup_inputs():
    n = np.random.standard_normal
    idx = np.random.permutation(T)[:I]
    idx2 = np.random.permutation(U)[:G]
    fd = mx_kscale(D)
    sensep = pack_weight(n((D, T)) / fd[:, None], "e4m3")
    return {
        "hid": (n((D, Q)) * 1.0 / np.sqrt(D) * fd[:, None]).astype(np.float32),
        "sense_words": sensep[0],
        "sense_scales": sensep[1],
        "wbias": np.tile(0.5 * n(U), (128, 1)).astype(np.float32),
        "offs": striped(idx),
        "offs2": striped(idx2),
    }


def reference(hid, sense_words, sense_scales, wbias, offs, offs2):
    idx = unstriped(offs)
    idx2 = unstriped(offs2)
    senseu = unpack_weight(sense_words, sense_scales, "e4m3")
    hidq = mxq(f64(hid), 0, "e4m3")
    senseidxg = senseu[:, idx]
    a = hidq.T @ senseidxg
    s = np.log(np.exp(a).reshape(Q, G, I // G).sum(axis=2)) + f64(wbias)[:1][:, idx2]
    r = s - np.max(s, axis=1, keepdims=True)
    y = r - np.log(np.sum(np.exp(r), axis=1, keepdims=True))
    return y

@@ -1,0 +1,154 @@
+from contextlib import ExitStack
+
+import concourse.mybir as mybir
+
+D, T, I, G, U, Q = 512, 4096, 2048, 512, 1024, 128
+FLOPS = 2 * D * Q * I
+
+F32 = mybir.dt.float32
+BF16 = mybir.dt.bfloat16
+I32 = mybir.dt.int32
+U32 = mybir.dt.uint32
+U16 = mybir.dt.uint16
+U8 = mybir.dt.uint8
+FP8X4 = mybir.dt.float8_e4m3fn_x4
+ALU = mybir.AluOpType
+ACT = mybir.ActivationFunctionType
+AX = mybir.AxisListType
+
+P = 128
+PACK = 4
+SENSES = I // G
+SLOTS = 512
+CHUNKS = I // SLOTS
+WORDS = SLOTS // SENSES
+QUAD = 32
+
+
+def tile_attend_sensesum_kernel(tc, hid, sense_words, sense_scales, wbias, offs, offs2, out):
+    nc = tc.nc
+    with ExitStack() as ctx:
+        sb = ctx.enter_context(tc.tile_pool(name="sb", bufs=1))
+        ps = ctx.enter_context(tc.psum_pool(name="ps", bufs=1))
+
+        slot_list = sb.tile([P, I // 16], U16, name="slot_list")
+        word_list = sb.tile([P, G // 16], U16, name="word_list")
+        store_words = sb.tile([P, T], I32, name="store_words", align_bytes=64)
+        store_scales = sb.tile([P, T], U8, name="store_scales", align_bytes=64)
+        bias_table = sb.tile([P, U], F32, name="bias_table", align_bytes=64)
+        hid_raw = sb.tile([P, PACK, Q], F32, name="hid_raw", align_bytes=64)
+
+        nc.vector.memset(store_scales[:].bitcast(I32), 0)
+        nc.vector.memset(bias_table[0 : P - QUAD, :], 0.0)
+
+        nc.sync.dma_start(word_list[:], offs2)
+        nc.sync.dma_start(bias_table[P - QUAD : P, :], wbias[P - QUAD : P, :])
+        nc.sync.dma_start(slot_list[:], offs)
+        for quad in range(4):
+            nc.sync.dma_start(
+                store_scales[QUAD * quad : QUAD * quad + 4, :].bitcast(I32),
+                sense_scales[0, 4 * quad : 4 * quad + 4, :].bitcast(I32),
+            )
+        nc.sync.dma_start(hid_raw[:], hid.rearrange("(p j) q -> p j q", j=PACK))
+        nc.sync.dma_start(store_words[:], sense_words[0].rearrange("p t r -> p (t r)").bitcast(I32))
+
+        bias_picked = sb.tile([P, G], F32, name="bias_picked", align_bytes=64)
+        nc.vector.tensor_copy(bias_picked[:], bias_table[:].indirect(word_list[:]))
+        bias = sb.tile([P, G], F32, name="bias", align_bytes=64)
+        for quad in range(4):
+            nc.sync.dma_start(bias[QUAD * quad : QUAD * (quad + 1), :], bias_picked[P - QUAD : P, :])
+
+        hid_bf = sb.tile([P, Q, PACK], BF16, name="hid_bf", align_bytes=64)
+        nc.scalar.activation(hid_bf[:], hid_raw[:].rearrange("p j q -> p q j"), ACT.Copy)
+        hid_codes = sb.tile([P, Q], U32, name="hid_codes", align_bytes=64)
+        hid_scales = sb.tile([P, Q], U8, name="hid_scales", align_bytes=64)
+
+        cols = SLOTS // 16
+        picked_scales = sb.tile([P, I], U8, name="picked_scales", align_bytes=64)
+        nc.vector.tensor_copy(picked_scales[:], store_scales[:].indirect(slot_list[:]))
+        nc.vector.quantize_mx(
+            out=hid_codes[:].bitcast(FP8X4),
+            scales=hid_scales[:],
+            in_=hid_bf[:].rearrange("p q j -> p (q j)"),
+        )
+
+        scores = []
+        for k in range(CHUNKS):
+            picked_words = sb.tile([P, SLOTS], U32, name="picked_words%d" % k, align_bytes=64)
+            nc.vector.tensor_copy(
+                picked_words[:], store_words[:].bitcast(U32).indirect(slot_list[:, k * cols : (k + 1) * cols])
+            )
+            score = ps.tile([P, SLOTS], F32, name="score%d" % k)
+            nc.tensor.matmul_mx(
+                out=score[:],
+                lhsT=hid_codes[:].bitcast(FP8X4),
+                lhsT_scale=hid_scales[:],
+                rhs=picked_words[:].bitcast(FP8X4),
+                rhs_scale=picked_scales[:, k * SLOTS : (k + 1) * SLOTS],
+                start=True,
+                stop=True,
+            )
+            scores.append(score)
+
+        neg_top = sb.tile([P, G], F32, name="neg_top", align_bytes=64)
+        expd = sb.tile([P, SENSES, G], F32, name="expd", align_bytes=64)
+
+        def word_top(k):
+            nc.vector.tensor_reduce(
+                neg_top[:, k * WORDS : (k + 1) * WORDS],
+                scores[k][:].rearrange("p (g j) -> p g j", j=SENSES),
+                AX.X,
+                ALU.max,
+                negate=True,
+            )
+
+        def shifted_exp(k):
+            words = slice(k * WORDS, (k + 1) * WORDS)
+            shifted = sb.tile([P, SENSES, WORDS], F32, name="shifted%d" % k, align_bytes=64)
+            nc.vector.tensor_tensor(
+                shifted[:],
+                scores[k][:].rearrange("p (g j) -> p j g", j=SENSES),
+                neg_top[:, words].unsqueeze(1).to_broadcast([P, SENSES, WORDS]),
+                ALU.add,
+            )
+            nc.scalar.activation(expd[:, :, words], shifted[:], ACT.Exp)
+
+        for k in range(CHUNKS):
+            word_top(k)
+        shifted_exp(0)
+        neg_base = sb.tile([P, G], F32, name="neg_base", align_bytes=64)
+        nc.vector.tensor_tensor(neg_base[:], neg_top[:], bias[:], ALU.subtract)
+        shifted_exp(1)
+        neg_row_top = sb.tile([P, 1], F32, name="neg_row_top")
+        nc.vector.tensor_reduce(neg_row_top[:], neg_base[:], AX.X, ALU.min)
+        weight = sb.tile([P, G], F32, name="weight", align_bytes=64)
+        nc.scalar.activation(weight[:], neg_base[:], ACT.Exp, bias=neg_row_top[:], scale=-1.0)
+        shifted_exp(2)
+        shifted_exp(3)
+
+        pairs = sb.tile([P, 2, G], F32, name="pairs", align_bytes=64)
+        sums = sb.tile([P, G], F32, name="sums", align_bytes=64)
+        early = slice(0, G - WORDS)
+        late = slice(G - WORDS, G)
+        nc.vector.tensor_tensor(pairs[:, :, early], expd[:, 0:2, early], expd[:, 2:4, early], ALU.add)
+        nc.vector.tensor_tensor(pairs[:, :, late], expd[:, 0:2, late], expd[:, 2:4, late], ALU.add)
+        nc.vector.tensor_tensor(sums[:], pairs[:, 0, :], pairs[:, 1, :], ALU.add)
+
+        weighted = sb.tile([P, G], F32, name="weighted", align_bytes=64)
+        total = sb.tile([P, 1], F32, name="total")
+        nc.vector.scalar_tensor_tensor(
+            weighted[:], sums[:], 1.0, weight[:], ALU.mult, ALU.mult, accum_out=total[:]
+        )
+        inv_total = sb.tile([P, 1], F32, name="inv_total")
+        nc.vector.reciprocal(inv_total[:], total[:])
+
+        half = G // 2
+        for h in range(2):
+            part = slice(h * half, (h + 1) * half)
+            logs = sb.tile([P, half], F32, name="logs%d" % h, align_bytes=64)
+            nc.scalar.activation(logs[:], sums[:, part], ACT.Ln, scale=inv_total[:])
+            result = sb.tile([P, half], F32, name="result%d" % h, align_bytes=64)
+            nc.vector.scalar_tensor_tensor(
+                result[:], logs[:], neg_row_top[:], neg_base[:, part], ALU.add, ALU.subtract
+            )
+            nc.sync.dma_start(out[:, part], result[:])

@@ -1,6 +1,7 @@
 from contextlib import ExitStack
 
 import concourse.mybir as mybir
+from concourse.masks import make_identity
 
 D, T, I, G, U, Q = 512, 4096, 2048, 512, 1024, 128
 FLOPS = 2 * D * Q * I
@@ -72,13 +73,21 @@ def tile_attend_sensesum_kernel(tc, hid, sense_words, sense_scales, wbias, offs,
             in_=hid_bf[:].rearrange("p q j -> p (q j)"),
         )
 
+        identity = sb.tile([P, P], F32, name="identity", align_bytes=64)
+        make_identity(nc, identity[:])
+
+        last = CHUNKS - 1
         scores = []
-        for k in range(CHUNKS):
-            picked_words = sb.tile([P, SLOTS], U32, name="picked_words%d" % k, align_bytes=64)
+        dealt = []
+        turned_exp = []
+        neg_top = sb.tile([P, G], F32, name="neg_top", align_bytes=64)
+
+        def score_chunk(k):
+            picked_words = sb.tile([P, SLOTS], U32, name="picked_words", align_bytes=64, bufs=2)
             nc.vector.tensor_copy(
                 picked_words[:], store_words[:].bitcast(U32).indirect(slot_list[:, k * cols : (k + 1) * cols])
             )
-            score = ps.tile([P, SLOTS], F32, name="score%d" % k)
+            score = ps.tile([P, SLOTS], F32, name="score%d" % k, tag="bank%d" % k)
             nc.tensor.matmul_mx(
                 out=score[:],
                 lhsT=hid_codes[:].bitcast(FP8X4),
@@ -89,9 +98,10 @@ def tile_attend_sensesum_kernel(tc, hid, sense_words, sense_scales, wbias, offs,
                 stop=True,
             )
             scores.append(score)
-
-        neg_top = sb.tile([P, G], F32, name="neg_top", align_bytes=64)
-        expd = sb.tile([P, SENSES, G], F32, name="expd", align_bytes=64)
+            if k < last:
+                by_sense = sb.tile([P, SENSES, WORDS], F32, name="by_sense%d" % k, align_bytes=64)
+                nc.scalar.copy(by_sense[:], score[:].rearrange("p (g j) -> p j g", j=SENSES))
+                dealt.append(by_sense)
 
         def word_top(k):
             nc.vector.tensor_reduce(
@@ -102,53 +112,88 @@ def tile_attend_sensesum_kernel(tc, hid, sense_words, sense_scales, wbias, offs,
                 negate=True,
             )
 
-        def shifted_exp(k):
-            words = slice(k * WORDS, (k + 1) * WORDS)
-            shifted = sb.tile([P, SENSES, WORDS], F32, name="shifted%d" % k, align_bytes=64)
-            nc.vector.tensor_tensor(
-                shifted[:],
-                scores[k][:].rearrange("p (g j) -> p j g", j=SENSES),
-                neg_top[:, words].unsqueeze(1).to_broadcast([P, SENSES, WORDS]),
-                ALU.add,
-            )
-            nc.scalar.activation(expd[:, :, words], shifted[:], ACT.Exp)
+        def turned_shifted_exp(k):
+            turned = ps.tile([P, SENSES, Q], F32, name="turned%d" % k, tag="turn%d" % k)
+            for j in range(SENSES):
+                nc.tensor.matmul(
+                    turned[:, j, :], dealt[k][:, j, :], identity[:], start=True, stop=False, is_transpose=True
+                )
+                nc.tensor.matmul(
+                    turned[:, j, :],
+                    neg_top[:, k * WORDS : (k + 1) * WORDS],
+                    identity[:],
+                    start=False,
+                    stop=True,
+                    is_transpose=True,
+                )
+            expd = sb.tile([P, SENSES, Q], F32, name="expd%d" % k, align_bytes=64)
+            nc.scalar.activation(expd[:], turned[:], ACT.Exp)
+            turned_exp.append(expd)
 
-        for k in range(CHUNKS):
+        score_chunk(0)
+        score_chunk(1)
+        for k in range(last):
             word_top(k)
-        shifted_exp(0)
-        neg_base = sb.tile([P, G], F32, name="neg_base", align_bytes=64)
-        nc.vector.tensor_tensor(neg_base[:], neg_top[:], bias[:], ALU.subtract)
-        shifted_exp(1)
-        neg_row_top = sb.tile([P, 1], F32, name="neg_row_top")
-        nc.vector.tensor_reduce(neg_row_top[:], neg_base[:], AX.X, ALU.min)
-        weight = sb.tile([P, G], F32, name="weight", align_bytes=64)
-        nc.scalar.activation(weight[:], neg_base[:], ACT.Exp, bias=neg_row_top[:], scale=-1.0)
-        shifted_exp(2)
-        shifted_exp(3)
+            if k + 2 < CHUNKS:
+                score_chunk(k + 2)
+            turned_shifted_exp(k)
+        word_top(last)
 
-        pairs = sb.tile([P, 2, G], F32, name="pairs", align_bytes=64)
-        sums = sb.tile([P, G], F32, name="sums", align_bytes=64)
         early = slice(0, G - WORDS)
         late = slice(G - WORDS, G)
-        nc.vector.tensor_tensor(pairs[:, :, early], expd[:, 0:2, early], expd[:, 2:4, early], ALU.add)
-        nc.vector.tensor_tensor(pairs[:, :, late], expd[:, 0:2, late], expd[:, 2:4, late], ALU.add)
-        nc.vector.tensor_tensor(sums[:], pairs[:, 0, :], pairs[:, 1, :], ALU.add)
-
-        weighted = sb.tile([P, G], F32, name="weighted", align_bytes=64)
-        total = sb.tile([P, 1], F32, name="total")
-        nc.vector.scalar_tensor_tensor(
-            weighted[:], sums[:], 1.0, weight[:], ALU.mult, ALU.mult, accum_out=total[:]
+        neg_base = sb.tile([P, G], F32, name="neg_base", align_bytes=64)
+        nc.vector.tensor_tensor(neg_base[:], neg_top[:], bias[:], ALU.subtract)
+        shifted = sb.tile([P, WORDS, SENSES], F32, name="shifted", align_bytes=64)
+        nc.vector.tensor_tensor(
+            shifted[:],
+            scores[last][:].rearrange("p (g j) -> p g j", j=SENSES),
+            neg_top[:, late].unsqueeze(2).to_broadcast([P, WORDS, SENSES]),
+            ALU.add,
         )
+        neg_row_top = sb.tile([P, 1], F32, name="neg_row_top")
+        nc.vector.tensor_reduce(neg_row_top[:], neg_base[:], AX.X, ALU.min)
+        late_exp = sb.tile([P, WORDS, SENSES], F32, name="late_exp", align_bytes=64)
+        nc.scalar.activation(late_exp[:], shifted[:], ACT.Exp)
+        weight = sb.tile([P, G], F32, name="weight", align_bytes=64)
+        nc.scalar.activation(weight[:], neg_base[:], ACT.Exp, bias=neg_row_top[:], scale=-1.0)
+
+        early_sums = ps.tile([P, G - WORDS], F32, name="early_sums", tag="bank%d" % (last - 1))
+        for k in range(last):
+            for j in range(SENSES):
+                nc.tensor.matmul(
+                    early_sums[:, k * WORDS : (k + 1) * WORDS],
+                    turned_exp[k][:, j, :],
+                    identity[:],
+                    start=(j == 0),
+                    stop=(j == SENSES - 1),
+                    is_transpose=True,
+                )
+
+        late_sums = sb.tile([P, WORDS], F32, name="late_sums", align_bytes=64)
+        nc.vector.tensor_reduce(late_sums[:], late_exp[:], AX.X, ALU.add)
+        weighted = sb.tile([P, G], F32, name="weighted", align_bytes=64)
+        late_total = sb.tile([P, 1], F32, name="late_total")
+        early_total = sb.tile([P, 1], F32, name="early_total")
+        nc.vector.scalar_tensor_tensor(
+            weighted[:, early], early_sums[:], 1.0, weight[:, early], ALU.mult, ALU.mult, accum_out=early_total[:]
+        )
+        nc.vector.scalar_tensor_tensor(
+            weighted[:, late], late_sums[:], 1.0, weight[:, late], ALU.mult, ALU.mult, accum_out=late_total[:]
+        )
+        total = sb.tile([P, 1], F32, name="total")
+        nc.vector.tensor_tensor(total[:], early_total[:], late_total[:], ALU.add)
         inv_total = sb.tile([P, 1], F32, name="inv_total")
         nc.vector.reciprocal(inv_total[:], total[:])
 
-        half = G // 2
-        for h in range(2):
-            part = slice(h * half, (h + 1) * half)
-            logs = sb.tile([P, half], F32, name="logs%d" % h, align_bytes=64)
-            nc.scalar.activation(logs[:], sums[:, part], ACT.Ln, scale=inv_total[:])
-            result = sb.tile([P, half], F32, name="result%d" % h, align_bytes=64)
+        logs = sb.tile([P, G], F32, name="logs", align_bytes=64)
+        result = sb.tile([P, G], F32, name="result", align_bytes=64)
+        for k in range(CHUNKS):
+            part = slice(k * WORDS, (k + 1) * WORDS)
+            sums = early_sums[:, part] if k < last else late_sums[:]
+            nc.scalar.activation(logs[:, part], sums, ACT.Ln, scale=inv_total[:])
             nc.vector.scalar_tensor_tensor(
-                result[:], logs[:], neg_row_top[:], neg_base[:, part], ALU.add, ALU.subtract
+                result[:, part], logs[:, part], neg_row_top[:], neg_base[:, part], ALU.add, ALU.subtract
             )
-            nc.sync.dma_start(out[:, part], result[:])
+            if k % 2 == 1:
+                pair = slice((k - 1) * WORDS, (k + 1) * WORDS)
+                nc.sync.dma_start(out[:, pair], result[:, pair])

@@ -24,6 +24,7 @@ SLOTS = 512
 CHUNKS = I // SLOTS
 WORDS = SLOTS // SENSES
 QUAD = 32
+TURNED = 2
 
 
 def tile_attend_sensesum_kernel(tc, hid, sense_words, sense_scales, wbias, offs, offs2, out):
@@ -76,18 +77,18 @@ def tile_attend_sensesum_kernel(tc, hid, sense_words, sense_scales, wbias, offs,
         identity = sb.tile([P, P], F32, name="identity", align_bytes=64)
         make_identity(nc, identity[:])
 
-        last = CHUNKS - 1
         scores = []
         dealt = []
         turned_exp = []
         neg_top = sb.tile([P, G], F32, name="neg_top", align_bytes=64)
+        neg_base = sb.tile([P, G], F32, name="neg_base", align_bytes=64)
 
         def score_chunk(k):
             picked_words = sb.tile([P, SLOTS], U32, name="picked_words", align_bytes=64, bufs=2)
             nc.vector.tensor_copy(
                 picked_words[:], store_words[:].bitcast(U32).indirect(slot_list[:, k * cols : (k + 1) * cols])
             )
-            score = ps.tile([P, SLOTS], F32, name="score%d" % k, tag="bank%d" % k)
+            score = ps.tile([P, SLOTS], F32, name="score%d" % k)
             nc.tensor.matmul_mx(
                 out=score[:],
                 lhsT=hid_codes[:].bitcast(FP8X4),
@@ -98,22 +99,24 @@ def tile_attend_sensesum_kernel(tc, hid, sense_words, sense_scales, wbias, offs,
                 stop=True,
             )
             scores.append(score)
-            if k < last:
+            if k < TURNED:
                 by_sense = sb.tile([P, SENSES, WORDS], F32, name="by_sense%d" % k, align_bytes=64)
                 nc.scalar.copy(by_sense[:], score[:].rearrange("p (g j) -> p j g", j=SENSES))
                 dealt.append(by_sense)
 
         def word_top(k):
+            words = slice(k * WORDS, (k + 1) * WORDS)
             nc.vector.tensor_reduce(
-                neg_top[:, k * WORDS : (k + 1) * WORDS],
+                neg_top[:, words],
                 scores[k][:].rearrange("p (g j) -> p g j", j=SENSES),
                 AX.X,
                 ALU.max,
                 negate=True,
             )
+            nc.gpsimd.tensor_tensor(neg_base[:, words], neg_top[:, words], bias[:, words], ALU.subtract)
 
         def turned_shifted_exp(k):
-            turned = ps.tile([P, SENSES, Q], F32, name="turned%d" % k, tag="turn%d" % k)
+            turned = ps.tile([P, SENSES, Q], F32, name="turned%d" % k)
             for j in range(SENSES):
                 nc.tensor.matmul(
                     turned[:, j, :], dealt[k][:, j, :], identity[:], start=True, stop=False, is_transpose=True
@@ -130,35 +133,40 @@ def tile_attend_sensesum_kernel(tc, hid, sense_words, sense_scales, wbias, offs,
             nc.scalar.activation(expd[:], turned[:], ACT.Exp)
             turned_exp.append(expd)
 
+        straight_exp = []
+
+        def shifted_exp(k):
+            shifted = sb.tile([P, WORDS, SENSES], F32, name="shifted%d" % k, align_bytes=64)
+            nc.vector.tensor_tensor(
+                shifted[:],
+                scores[k][:].rearrange("p (g j) -> p g j", j=SENSES),
+                neg_top[:, k * WORDS : (k + 1) * WORDS].unsqueeze(2).to_broadcast([P, WORDS, SENSES]),
+                ALU.add,
+            )
+            expd = sb.tile([P, WORDS, SENSES], F32, name="expd%d" % k, align_bytes=64)
+            nc.scalar.activation(expd[:], shifted[:], ACT.Exp)
+            straight_exp.append(expd)
+
         score_chunk(0)
         score_chunk(1)
-        for k in range(last):
+        for k in range(TURNED):
             word_top(k)
-            if k + 2 < CHUNKS:
-                score_chunk(k + 2)
+            score_chunk(k + 2)
             turned_shifted_exp(k)
-        word_top(last)
+        for k in range(TURNED, CHUNKS):
+            word_top(k)
+            shifted_exp(k)
 
-        early = slice(0, G - WORDS)
-        late = slice(G - WORDS, G)
-        neg_base = sb.tile([P, G], F32, name="neg_base", align_bytes=64)
-        nc.vector.tensor_tensor(neg_base[:], neg_top[:], bias[:], ALU.subtract)
-        shifted = sb.tile([P, WORDS, SENSES], F32, name="shifted", align_bytes=64)
-        nc.vector.tensor_tensor(
-            shifted[:],
-            scores[last][:].rearrange("p (g j) -> p g j", j=SENSES),
-            neg_top[:, late].unsqueeze(2).to_broadcast([P, WORDS, SENSES]),
-            ALU.add,
-        )
         neg_row_top = sb.tile([P, 1], F32, name="neg_row_top")
         nc.vector.tensor_reduce(neg_row_top[:], neg_base[:], AX.X, ALU.min)
-        late_exp = sb.tile([P, WORDS, SENSES], F32, name="late_exp", align_bytes=64)
-        nc.scalar.activation(late_exp[:], shifted[:], ACT.Exp)
         weight = sb.tile([P, G], F32, name="weight", align_bytes=64)
         nc.scalar.activation(weight[:], neg_base[:], ACT.Exp, bias=neg_row_top[:], scale=-1.0)
 
-        early_sums = ps.tile([P, G - WORDS], F32, name="early_sums", tag="bank%d" % (last - 1))
-        for k in range(last):
+        split = TURNED * WORDS
+        early = slice(0, split)
+        late = slice(split, G)
+        early_sums = ps.tile([P, split], F32, name="early_sums", tag="score2")
+        for k in range(TURNED):
             for j in range(SENSES):
                 nc.tensor.matmul(
                     early_sums[:, k * WORDS : (k + 1) * WORDS],
@@ -168,9 +176,10 @@ def tile_attend_sensesum_kernel(tc, hid, sense_words, sense_scales, wbias, offs,
                     stop=(j == SENSES - 1),
                     is_transpose=True,
                 )
+        late_sums = sb.tile([P, G - split], F32, name="late_sums", align_bytes=64)
+        for k in range(CHUNKS - TURNED):
+            nc.vector.tensor_reduce(late_sums[:, k * WORDS : (k + 1) * WORDS], straight_exp[k][:], AX.X, ALU.add)
 
-        late_sums = sb.tile([P, WORDS], F32, name="late_sums", align_bytes=64)
-        nc.vector.tensor_reduce(late_sums[:], late_exp[:], AX.X, ALU.add)
         weighted = sb.tile([P, G], F32, name="weighted", align_bytes=64)
         late_total = sb.tile([P, 1], F32, name="late_total")
         early_total = sb.tile([P, 1], F32, name="early_total")
@@ -189,7 +198,10 @@ def tile_attend_sensesum_kernel(tc, hid, sense_words, sense_scales, wbias, offs,
         result = sb.tile([P, G], F32, name="result", align_bytes=64)
         for k in range(CHUNKS):
             part = slice(k * WORDS, (k + 1) * WORDS)
-            sums = early_sums[:, part] if k < last else late_sums[:]
+            if k < TURNED:
+                sums = early_sums[:, part]
+            else:
+                sums = late_sums[:, k * WORDS - split : (k + 1) * WORDS - split]
             nc.scalar.activation(logs[:, part], sums, ACT.Ln, scale=inv_total[:])
             nc.vector.scalar_tensor_tensor(
                 result[:, part], logs[:, part], neg_row_top[:], neg_base[:, part], ALU.add, ALU.subtract

@@ -46,10 +46,10 @@ def tile_attend_sensesum_kernel(tc, hid, sense_words, sense_scales, wbias, offs,
         nc.sync.dma_start(word_list[:], offs2)
         nc.sync.dma_start(bias_table[P - QUAD : P, :], wbias[P - QUAD : P, :])
         nc.sync.dma_start(slot_list[:], offs)
-        for quad in range(4):
+        for row in range(4):
             nc.sync.dma_start(
-                store_scales[QUAD * quad : QUAD * quad + 4, :].bitcast(I32),
-                sense_scales[0, 4 * quad : 4 * quad + 4, :].bitcast(I32),
+                store_scales[row:P:QUAD, :].bitcast(I32),
+                sense_scales[0, row:16:4, :].bitcast(I32),
             )
         nc.sync.dma_start(hid_raw[:], hid.rearrange("(p j) q -> p j q", j=PACK))
         nc.sync.dma_start(store_words[:], sense_words[0].rearrange("p t r -> p (t r)").bitcast(I32))
@@ -134,17 +134,26 @@ def tile_attend_sensesum_kernel(tc, hid, sense_words, sense_scales, wbias, offs,
             turned_exp.append(expd)
 
         straight_exp = []
+        half = WORDS // 2
 
-        def shifted_exp(k):
-            shifted = sb.tile([P, WORDS, SENSES], F32, name="shifted%d" % k, align_bytes=64)
-            nc.vector.tensor_tensor(
-                shifted[:],
-                scores[k][:].rearrange("p (g j) -> p g j", j=SENSES),
-                neg_top[:, k * WORDS : (k + 1) * WORDS].unsqueeze(2).to_broadcast([P, WORDS, SENSES]),
-                ALU.add,
-            )
-            expd = sb.tile([P, WORDS, SENSES], F32, name="expd%d" % k, align_bytes=64)
-            nc.scalar.activation(expd[:], shifted[:], ACT.Exp)
+        def straight_shifted_exp(k):
+            by_word = scores[k][:].rearrange("p (g j) -> p g j", j=SENSES)
+            halves = [(slice(h * half, (h + 1) * half), slice(k * WORDS + h * half, k * WORDS + (h + 1) * half)) for h in range(2)]
+            for local, words in halves:
+                nc.vector.tensor_reduce(neg_top[:, words], by_word[:, local, :], AX.X, ALU.max, negate=True)
+            words = slice(k * WORDS, (k + 1) * WORDS)
+            nc.gpsimd.tensor_tensor(neg_base[:, words], neg_top[:, words], bias[:, words], ALU.subtract)
+            by_sense = scores[k][:].rearrange("p (g j) -> p j g", j=SENSES)
+            shifted = sb.tile([P, 2, SENSES, half], F32, name="shifted%d" % k, align_bytes=64)
+            expd = sb.tile([P, SENSES, WORDS], F32, name="expd%d" % k, align_bytes=64)
+            for h, (local, words) in enumerate(halves):
+                nc.vector.tensor_tensor(
+                    shifted[:, h, :, :],
+                    by_sense[:, :, local],
+                    neg_top[:, words].unsqueeze(1).to_broadcast([P, SENSES, half]),
+                    ALU.add,
+                )
+                nc.scalar.activation(expd[:, :, local], shifted[:, h, :, :], ACT.Exp)
             straight_exp.append(expd)
 
         score_chunk(0)
@@ -154,8 +163,7 @@ def tile_attend_sensesum_kernel(tc, hid, sense_words, sense_scales, wbias, offs,
             score_chunk(k + 2)
             turned_shifted_exp(k)
         for k in range(TURNED, CHUNKS):
-            word_top(k)
-            shifted_exp(k)
+            straight_shifted_exp(k)
 
         neg_row_top = sb.tile([P, 1], F32, name="neg_row_top")
         nc.vector.tensor_reduce(neg_row_top[:], neg_base[:], AX.X, ALU.min)
@@ -177,12 +185,15 @@ def tile_attend_sensesum_kernel(tc, hid, sense_words, sense_scales, wbias, offs,
                     is_transpose=True,
                 )
         late_sums = sb.tile([P, G - split], F32, name="late_sums", align_bytes=64)
-        for k in range(CHUNKS - TURNED):
-            nc.vector.tensor_reduce(late_sums[:, k * WORDS : (k + 1) * WORDS], straight_exp[k][:], AX.X, ALU.add)
+        pairs = sb.tile([P, 2, 2, WORDS], F32, name="pairs", align_bytes=64)
+        nc.gpsimd.tensor_tensor(pairs[:, 0], straight_exp[0][:, 0:2, :], straight_exp[0][:, 2:4, :], ALU.add)
+        nc.gpsimd.tensor_tensor(late_sums[:, 0:WORDS], pairs[:, 0, 0, :], pairs[:, 0, 1, :], ALU.add)
 
         weighted = sb.tile([P, G], F32, name="weighted", align_bytes=64)
         late_total = sb.tile([P, 1], F32, name="late_total")
         early_total = sb.tile([P, 1], F32, name="early_total")
+        nc.vector.tensor_tensor(pairs[:, 1], straight_exp[1][:, 0:2, :], straight_exp[1][:, 2:4, :], ALU.add)
+        nc.vector.tensor_tensor(late_sums[:, WORDS : 2 * WORDS], pairs[:, 1, 0, :], pairs[:, 1, 1, :], ALU.add)
         nc.vector.scalar_tensor_tensor(
             weighted[:, early], early_sums[:], 1.0, weight[:, early], ALU.mult, ALU.mult, accum_out=early_total[:]
         )

from contextlib import ExitStack

import concourse.mybir as mybir
from concourse.masks import make_identity

D, T, I, G, U, Q = 512, 4096, 2048, 512, 1024, 128
FLOPS = 2 * D * Q * I

F32 = mybir.dt.float32
BF16 = mybir.dt.bfloat16
I32 = mybir.dt.int32
U32 = mybir.dt.uint32
U16 = mybir.dt.uint16
U8 = mybir.dt.uint8
FP8X4 = mybir.dt.float8_e4m3fn_x4
ALU = mybir.AluOpType
ACT = mybir.ActivationFunctionType
AX = mybir.AxisListType

P = 128
PACK = 4
SENSES = I // G
SLOTS = 512
CHUNKS = I // SLOTS
WORDS = SLOTS // SENSES
QUAD = 32
TURNED = 2


def tile_attend_sensesum_kernel(tc, hid, sense_words, sense_scales, wbias, offs, offs2, out):
    nc = tc.nc
    with ExitStack() as ctx:
        sb = ctx.enter_context(tc.tile_pool(name="sb", bufs=1))
        ps = ctx.enter_context(tc.psum_pool(name="ps", bufs=1))

        slot_list = sb.tile([P, I // 16], U16, name="slot_list")
        word_list = sb.tile([P, G // 16], U16, name="word_list")
        store_words = sb.tile([P, T], I32, name="store_words", align_bytes=64)
        store_scales = sb.tile([P, T], U8, name="store_scales", align_bytes=64)
        bias_table = sb.tile([P, U], F32, name="bias_table", align_bytes=64)
        hid_raw = sb.tile([P, PACK, Q], F32, name="hid_raw", align_bytes=64)

        nc.vector.memset(store_scales[:].bitcast(I32), 0)
        nc.vector.memset(bias_table[0 : P - QUAD, :], 0.0)

        nc.sync.dma_start(word_list[:], offs2)
        nc.sync.dma_start(bias_table[P - QUAD : P, :], wbias[P - QUAD : P, :])
        nc.sync.dma_start(slot_list[:], offs)
        for row in range(4):
            nc.sync.dma_start(
                store_scales[row:P:QUAD, :].bitcast(I32),
                sense_scales[0, row:16:4, :].bitcast(I32),
            )
        nc.sync.dma_start(hid_raw[:], hid.rearrange("(p j) q -> p j q", j=PACK))
        nc.sync.dma_start(store_words[:], sense_words[0].rearrange("p t r -> p (t r)").bitcast(I32))

        bias_picked = sb.tile([P, G], F32, name="bias_picked", align_bytes=64)
        nc.vector.tensor_copy(bias_picked[:], bias_table[:].indirect(word_list[:]))
        bias = sb.tile([P, G], F32, name="bias", align_bytes=64)
        for quad in range(4):
            nc.sync.dma_start(bias[QUAD * quad : QUAD * (quad + 1), :], bias_picked[P - QUAD : P, :])

        hid_bf = sb.tile([P, Q, PACK], BF16, name="hid_bf", align_bytes=64)
        nc.scalar.activation(hid_bf[:], hid_raw[:].rearrange("p j q -> p q j"), ACT.Copy)
        hid_codes = sb.tile([P, Q], U32, name="hid_codes", align_bytes=64)
        hid_scales = sb.tile([P, Q], U8, name="hid_scales", align_bytes=64)

        cols = SLOTS // 16
        picked_scales = sb.tile([P, I], U8, name="picked_scales", align_bytes=64)
        nc.vector.tensor_copy(picked_scales[:], store_scales[:].indirect(slot_list[:]))
        nc.vector.quantize_mx(
            out=hid_codes[:].bitcast(FP8X4),
            scales=hid_scales[:],
            in_=hid_bf[:].rearrange("p q j -> p (q j)"),
        )

        identity = sb.tile([P, P], F32, name="identity", align_bytes=64)
        make_identity(nc, identity[:])

        scores = []
        dealt = []
        turned_exp = []
        neg_top = sb.tile([P, G], F32, name="neg_top", align_bytes=64)
        neg_base = sb.tile([P, G], F32, name="neg_base", align_bytes=64)

        def score_chunk(k):
            picked_words = sb.tile([P, SLOTS], U32, name="picked_words", align_bytes=64, bufs=2)
            nc.vector.tensor_copy(
                picked_words[:], store_words[:].bitcast(U32).indirect(slot_list[:, k * cols : (k + 1) * cols])
            )
            score = ps.tile([P, SLOTS], F32, name="score%d" % k)
            nc.tensor.matmul_mx(
                out=score[:],
                lhsT=hid_codes[:].bitcast(FP8X4),
                lhsT_scale=hid_scales[:],
                rhs=picked_words[:].bitcast(FP8X4),
                rhs_scale=picked_scales[:, k * SLOTS : (k + 1) * SLOTS],
                start=True,
                stop=True,
            )
            scores.append(score)
            if k < TURNED:
                by_sense = sb.tile([P, SENSES, WORDS], F32, name="by_sense%d" % k, align_bytes=64)
                nc.scalar.copy(by_sense[:], score[:].rearrange("p (g j) -> p j g", j=SENSES))
                dealt.append(by_sense)

        def word_top(k):
            words = slice(k * WORDS, (k + 1) * WORDS)
            nc.vector.tensor_reduce(
                neg_top[:, words],
                scores[k][:].rearrange("p (g j) -> p g j", j=SENSES),
                AX.X,
                ALU.max,
                negate=True,
            )
            nc.gpsimd.tensor_tensor(neg_base[:, words], neg_top[:, words], bias[:, words], ALU.subtract)

        def turned_shifted_exp(k):
            turned = ps.tile([P, SENSES, Q], F32, name="turned%d" % k)
            for j in range(SENSES):
                nc.tensor.matmul(
                    turned[:, j, :], dealt[k][:, j, :], identity[:], start=True, stop=False, is_transpose=True
                )
                nc.tensor.matmul(
                    turned[:, j, :],
                    neg_top[:, k * WORDS : (k + 1) * WORDS],
                    identity[:],
                    start=False,
                    stop=True,
                    is_transpose=True,
                )
            expd = sb.tile([P, SENSES, Q], F32, name="expd%d" % k, align_bytes=64)
            nc.scalar.activation(expd[:], turned[:], ACT.Exp)
            turned_exp.append(expd)

        straight_exp = []
        half = WORDS // 2

        def straight_shifted_exp(k):
            by_word = scores[k][:].rearrange("p (g j) -> p g j", j=SENSES)
            halves = [(slice(h * half, (h + 1) * half), slice(k * WORDS + h * half, k * WORDS + (h + 1) * half)) for h in range(2)]
            for local, words in halves:
                nc.vector.tensor_reduce(neg_top[:, words], by_word[:, local, :], AX.X, ALU.max, negate=True)
            words = slice(k * WORDS, (k + 1) * WORDS)
            nc.gpsimd.tensor_tensor(neg_base[:, words], neg_top[:, words], bias[:, words], ALU.subtract)
            by_sense = scores[k][:].rearrange("p (g j) -> p j g", j=SENSES)
            shifted = sb.tile([P, 2, SENSES, half], F32, name="shifted%d" % k, align_bytes=64)
            expd = sb.tile([P, SENSES, WORDS], F32, name="expd%d" % k, align_bytes=64)
            for h, (local, words) in enumerate(halves):
                nc.vector.tensor_tensor(
                    shifted[:, h, :, :],
                    by_sense[:, :, local],
                    neg_top[:, words].unsqueeze(1).to_broadcast([P, SENSES, half]),
                    ALU.add,
                )
                nc.scalar.activation(expd[:, :, local], shifted[:, h, :, :], ACT.Exp)
            straight_exp.append(expd)

        score_chunk(0)
        score_chunk(1)
        for k in range(TURNED):
            word_top(k)
            score_chunk(k + 2)
            turned_shifted_exp(k)
        for k in range(TURNED, CHUNKS):
            straight_shifted_exp(k)

        neg_row_top = sb.tile([P, 1], F32, name="neg_row_top")
        nc.vector.tensor_reduce(neg_row_top[:], neg_base[:], AX.X, ALU.min)
        weight = sb.tile([P, G], F32, name="weight", align_bytes=64)
        nc.scalar.activation(weight[:], neg_base[:], ACT.Exp, bias=neg_row_top[:], scale=-1.0)

        split = TURNED * WORDS
        early = slice(0, split)
        late = slice(split, G)
        early_sums = ps.tile([P, split], F32, name="early_sums", tag="score2")
        for k in range(TURNED):
            for j in range(SENSES):
                nc.tensor.matmul(
                    early_sums[:, k * WORDS : (k + 1) * WORDS],
                    turned_exp[k][:, j, :],
                    identity[:],
                    start=(j == 0),
                    stop=(j == SENSES - 1),
                    is_transpose=True,
                )
        late_sums = sb.tile([P, G - split], F32, name="late_sums", align_bytes=64)
        pairs = sb.tile([P, 2, 2, WORDS], F32, name="pairs", align_bytes=64)
        nc.gpsimd.tensor_tensor(pairs[:, 0], straight_exp[0][:, 0:2, :], straight_exp[0][:, 2:4, :], ALU.add)
        nc.gpsimd.tensor_tensor(late_sums[:, 0:WORDS], pairs[:, 0, 0, :], pairs[:, 0, 1, :], ALU.add)

        weighted = sb.tile([P, G], F32, name="weighted", align_bytes=64)
        late_total = sb.tile([P, 1], F32, name="late_total")
        early_total = sb.tile([P, 1], F32, name="early_total")
        nc.vector.tensor_tensor(pairs[:, 1], straight_exp[1][:, 0:2, :], straight_exp[1][:, 2:4, :], ALU.add)
        nc.vector.tensor_tensor(late_sums[:, WORDS : 2 * WORDS], pairs[:, 1, 0, :], pairs[:, 1, 1, :], ALU.add)
        nc.vector.scalar_tensor_tensor(
            weighted[:, early], early_sums[:], 1.0, weight[:, early], ALU.mult, ALU.mult, accum_out=early_total[:]
        )
        nc.vector.scalar_tensor_tensor(
            weighted[:, late], late_sums[:], 1.0, weight[:, late], ALU.mult, ALU.mult, accum_out=late_total[:]
        )
        total = sb.tile([P, 1], F32, name="total")
        nc.vector.tensor_tensor(total[:], early_total[:], late_total[:], ALU.add)
        inv_total = sb.tile([P, 1], F32, name="inv_total")
        nc.vector.reciprocal(inv_total[:], total[:])

        logs = sb.tile([P, G], F32, name="logs", align_bytes=64)
        result = sb.tile([P, G], F32, name="result", align_bytes=64)
        for k in range(CHUNKS):
            part = slice(k * WORDS, (k + 1) * WORDS)
            if k < TURNED:
                sums = early_sums[:, part]
            else:
                sums = late_sums[:, k * WORDS - split : (k + 1) * WORDS - split]
            nc.scalar.activation(logs[:, part], sums, ACT.Ln, scale=inv_total[:])
            nc.vector.scalar_tensor_tensor(
                result[:, part], logs[:, part], neg_row_top[:], neg_base[:, part], ALU.add, ALU.subtract
            )
            if k % 2 == 1:
                pair = slice((k - 1) * WORDS, (k + 1) * WORDS)
                nc.sync.dma_start(out[:, pair], result[:, pair])
